import numpy as np
import ml_dtypes


def mxq(x, axis, fmt="e4m3"):
    dtype, down = {"e4m3": (ml_dtypes.float8_e4m3fn, 7), "e5m2": (ml_dtypes.float8_e5m2, 14)}[fmt]
    v = np.moveaxis(np.asarray(x, np.float32).astype(ml_dtypes.bfloat16).astype(np.float64), axis, -1)
    blocks = v.reshape(v.shape[:-1] + (-1, 32))
    amax = np.abs(blocks).max(-1, keepdims=True)
    byte = np.maximum(np.where(amax > 0, np.frexp(amax)[1] - 1 + 127, 0) - down, 1)
    scale = np.exp2(byte - 127.0)
    codes = (blocks / scale).astype(np.float32).astype(dtype).astype(np.float64)
    return np.moveaxis((codes * scale).reshape(v.shape), -1, axis)


WIDE = False


def mx_kscale(k):
    if not WIDE:
        return np.ones(k)
    levels = np.array([30, -30])
    if k % 512:
        return np.exp2(np.random.permutation(np.resize(levels, k // 32))).repeat(32)
    a = np.empty((k // 512, 16))
    for p in range(k // 512):
        a[p, :8] = np.random.permutation(np.resize(levels, 8))
        for g in range(8):
            far = levels[np.abs(levels - a[p, g]) >= 10]
            a[p, g + 8] = far[np.random.randint(len(far))]
    return np.exp2(a.ravel()).repeat(32)


def f64(x):
    return np.asarray(x).astype(np.float64)


def striped(idx):
    return np.tile(idx.reshape(-1, 16).T, (8, 1)).astype(np.uint16)


def unstriped(offs):
    return offs[:16].T.reshape(-1).astype(np.int64)


E2M1 = np.array([0.0, 0.5, 1.0, 1.5, 2.0, 3.0, 4.0, 6.0, -0.0, -0.5, -1.0, -1.5, -2.0, -3.0, -4.0, -6.0])


def pack_weight(w, fmt):
    k, n = w.shape
    w = f64(np.asarray(w, np.float32).astype(ml_dtypes.bfloat16)).reshape(k // 32, 32, n)
    amax = np.abs(w).max(1)
    if fmt == "e4m3":
        byte = np.frexp(amax)[1] - 1 + 127 - 7
    elif fmt == "e5m2":
        byte = np.frexp(amax)[1] - 1 + 127 - 14
    else:
        mant, ex = np.frexp(amax / 6.0)
        byte = np.where(mant > 0.5, ex, ex - 1) + 127
    byte = np.clip(np.where(amax > 0, byte, 1), 1, 254)
    scaled = (w * np.exp2(127.0 - byte)[:, None, :]).reshape(k, n).astype(np.float32)
    by_word = np.ascontiguousarray(scaled.reshape(k // 512, 128, 4, n).transpose(0, 1, 3, 2))
    if fmt == "e4m3":
        words = by_word.astype(ml_dtypes.float8_e4m3fn).view(np.uint8)
    elif fmt == "e5m2":
        words = by_word.astype(ml_dtypes.float8_e5m2).view(np.uint8)
    else:
        c = by_word.astype(ml_dtypes.float4_e2m1fn).view(np.uint8) & 0xF
        words = (c[..., 0::2] | (c[..., 1::2] << 4)).reshape(k // 512, 128, 2 * n)
    return np.ascontiguousarray(words), np.ascontiguousarray(byte.astype(np.uint8).reshape(k // 512, 16, n))


def unpack_weight(words, scales, fmt):
    g, _, n = scales.shape
    words = np.ascontiguousarray(words).reshape(g, 128, n, -1)
    if fmt == "e4m3":
        vals = words.view(ml_dtypes.float8_e4m3fn).astype(np.float64)
    elif fmt == "e5m2":
        vals = words.view(ml_dtypes.float8_e5m2).astype(np.float64)
    else:
        nib = np.empty((g, 128, n, 4), np.uint8)
        nib[..., 0::2] = words & 0xF
        nib[..., 1::2] = words >> 4
        vals = E2M1[nib]
    vals = vals * np.repeat(np.exp2(scales.astype(np.float64) - 127.0), 8, axis=1)[..., None]
    return vals.transpose(0, 1, 3, 2).reshape(g * 512, n)


def sigmoid(v):
    return 1.0 / (1.0 + np.exp(-np.maximum(v, -700.0)))


def d_sigmoid(v):
    s = 1.0 / (1.0 + np.exp(-np.maximum(v, -700.0)))
    return s * (1.0 - s)


K, T, E, C, H, N = 128, 1024, 4, 512, 1024, 512


def by_expert(wq, xq):
    return np.concatenate([wq[e].T @ xq[:, e * C:(e + 1) * C] for e in range(E)], axis=1)


def setup_inputs():
    n = np.random.standard_normal
    s = mx_kscale(N)[:, None]
    u = mx_kscale(H)
    first = np.random.permutation(np.repeat(np.arange(E), T // E))
    second = (first + 1 + np.random.permutation(np.repeat(np.arange(E - 1), -(-T // (E - 1)))[:T])) % E
    while np.bincount(second, minlength=E).max() != T // E:
        load = np.bincount(second, minlength=E); hi, lo = int(load.argmax()), int(load.argmin())
        t = np.flatnonzero((second == hi) & (first != lo))[0]; second[t] = lo
    slot_token = np.empty(E * C, np.int64); pos = np.empty((2, T), np.int64); fill = np.zeros(E, np.int64)
    place = np.stack([np.random.permutation(C) for _ in range(E)])
    for r, deal in enumerate((first, second)):
        for t in np.random.permutation(T):
            e = deal[t]; j = e * C + place[e, fill[e]]; fill[e] += 1; slot_token[j] = t; pos[r, t] = j
    g = np.random.uniform(0.2, 0.8, T)
    w_slot = np.empty(E * C); w_slot[pos[0]] = g; w_slot[pos[1]] = 1.0 - g
    dy = pack_weight(n((N, T)) * s, "e5m2")
    w2 = [pack_weight(m, "e2m1") for m in n((E, N, H)) / np.sqrt(N) / s[None] * u[None, None, :]]
    w1 = [pack_weight(m, "e2m1") for m in n((E, H, K)) / np.sqrt(H) / u[None, :, None]]
    w3 = [pack_weight(m, "e2m1") for m in n((E, H, K)) / np.sqrt(H) / u[None, :, None]]
    return {
        "dy_words": dy[0],
        "dy_scales": dy[1],
        "a1": n((H, E * C)).astype(np.float32),
        "a3": n((H, E * C)).astype(np.float32),
        "w2_words": np.stack([m[0] for m in w2]),
        "w2_scales": np.stack([m[1] for m in w2]),
        "w1_words": np.stack([m[0] for m in w1]),
        "w1_scales": np.stack([m[1] for m in w1]),
        "w3_words": np.stack([m[0] for m in w3]),
        "w3_scales": np.stack([m[1] for m in w3]),
        "gate": np.tile(w_slot, (H, 1)).astype(np.float32),
        "offs": striped(slot_token),
        "pos1": striped(pos[0]),
        "pos2": striped(pos[1]),
    }


def reference(dy_words, dy_scales, a1, a3, w2_words, w2_scales, w1_words, w1_scales, w3_words, w3_scales, gate, offs, pos1, pos2):
    idx = unstriped(offs)
    w2 = np.stack([unpack_weight(w2_words[e], w2_scales[e], "e2m1") for e in range(E)])
    w1 = np.stack([unpack_weight(w1_words[e], w1_scales[e], "e2m1") for e in range(E)])
    w3 = np.stack([unpack_weight(w3_words[e], w3_scales[e], "e2m1") for e in range(E)])
    gq = unpack_weight(dy_words, dy_scales, "e5m2")[:, idx]
    dh = f64(gate) * by_expert(w2, gq)
    da1 = dh * f64(a3) * d_sigmoid(f64(a1))
    da3 = dh * sigmoid(f64(a1))
    dx = by_expert(w1, mxq(da1, 0, "e5m2")) + by_expert(w3, mxq(da3, 0, "e5m2"))
    return dx[:, unstriped(pos1)] + dx[:, unstriped(pos2)]

@@ -1,0 +1,264 @@
+from contextlib import ExitStack
+
+import concourse.mybir as mybir
+from concourse.masks import make_identity
+
+K, T, E, C, H, N = 128, 1024, 4, 512, 1024, 512
+SLOTS = E * C
+FLOPS = 2 * SLOTS * H * (N + 2 * K)
+BYTES = (N * T + N * T // 32 + 2 * 4 * H * SLOTS + E * H * (N + 2 * K) // 2 + E * H * (N + 2 * K) // 32
+         + 4 * SLOTS + 2 * 8 * (SLOTS + 2 * T) + 4 * K * T)
+
+F32 = mybir.dt.float32
+BF16 = mybir.dt.bfloat16
+I32 = mybir.dt.int32
+U32 = mybir.dt.uint32
+U16 = mybir.dt.uint16
+U8 = mybir.dt.uint8
+E5M2 = mybir.dt.float8_e5m2_x4
+E2M1 = mybir.dt.float4_e2m1fn_x4
+ACT = mybir.ActivationFunctionType
+ALU = mybir.AluOpType
+
+P = 128
+PACK = 4
+PASS = P * PACK
+HALVES = H // PASS
+UNITS = E * HALVES
+CHUNKS = C // P
+LIST_ROWS = 16
+D_ENG = "gsgsgsgsgsgsgsgsgsgsgsgsgsgsgsgs"
+W_ENG = "gvgvgvgvgvgvgvgvgvgvgvgvgvgvgvgv"
+OUT_PIECES = 2
+
+
+def tile_moe_bdx_glu_sigmoid_kernel(
+    tc, dy_words, dy_scales, a1, a3, w2_words, w2_scales, w1_words, w1_scales, w3_words, w3_scales,
+    gate, offs, pos1, pos2, out,
+):
+    nc = tc.nc
+    with ExitStack() as ctx:
+        keep = ctx.enter_context(tc.tile_pool(name="keep", bufs=1))
+        loads = ctx.enter_context(tc.tile_pool(name="loads", bufs=4))
+        work = ctx.enter_context(tc.tile_pool(name="work", bufs=6))
+        pairs = ctx.enter_context(tc.tile_pool(name="pairs", bufs=4))
+        unit_pool = ctx.enter_context(tc.tile_pool(name="unit", bufs=2))
+        psum_first = ctx.enter_context(tc.psum_pool(name="psum_first", bufs=3))
+        psum_dh = ctx.enter_context(tc.psum_pool(name="psum_dh", bufs=4))
+        psum_dx = ctx.enter_context(tc.psum_pool(name="psum_dx", bufs=1))
+
+        offs_sb = keep.tile([P, SLOTS // LIST_ROWS], U16, name="offs_sb")
+        pos1_sb = keep.tile([P, T // LIST_ROWS], U16, name="pos1_sb")
+        pos2_sb = keep.tile([P, T // LIST_ROWS], U16, name="pos2_sb")
+        dy_w = keep.tile([P, T], I32, name="dy_w", align_bytes=64)
+        dy_s = keep.tile([P, T], U8, name="dy_s", align_bytes=64)
+        w2_w = [keep.tile([P, 2 * H], U8, name="w2_w%d" % e, align_bytes=64) for e in range(E)]
+        w2_s = keep.tile([P, E, H], U8, name="w2_s", align_bytes=64)
+        w13_w = [keep.tile([P, UNITS, 2 * K], U8, name="w13_w%d" % m, align_bytes=64) for m in range(2)]
+        w13_s = [keep.tile([P, UNITS, K], U8, name="w13_s%d" % m, align_bytes=64) for m in range(2)]
+        g_w = [keep.tile([P, C], U32, name="g_w%d" % e, align_bytes=64) for e in range(E)]
+        g_s = [keep.tile([P, C], U8, name="g_s%d" % e, align_bytes=64) for e in range(E)]
+        ident = keep.tile([P, P], F32, name="ident")
+        gate_rows = keep.tile([P, P], F32, name="gate_rows")
+        gate_col = keep.tile([P, SLOTS // P], F32, name="gate_col")
+        minus_half = keep.tile([P, 1], F32, name="minus_half")
+        dx = keep.tile([P, SLOTS], F32, name="dx")
+
+        nc.vector.memset(dy_s[:].bitcast(I32), 0)
+        nc.vector.memset(w2_s[:].rearrange("p e i -> p (e i)").bitcast(I32), 0)
+        nc.vector.memset(gate_rows[:], 0.0)
+        nc.vector.memset(minus_half[:], -0.5)
+        for m in range(2):
+            nc.vector.memset(w13_s[m][:].rearrange("p u k -> p (u k)").bitcast(I32), 0)
+        make_identity(nc, ident[:])
+
+        a_tiles = {}
+
+        def load_saved(u, m):
+            e, h = divmod(u, HALVES)
+            tile = loads.tile([P, PACK, C], F32, name=("a1", "a3")[m])
+            rows = (a1, a3)[m][h * PASS : (h + 1) * PASS, e * C : (e + 1) * C]
+            nc.sync.dma_start(out=tile[:], in_=rows.rearrange("(p t) n -> p t n", t=PACK))
+            a_tiles[u, m] = tile
+
+        def load_unit(u):
+            load_saved(u, 0)
+            load_saved(u, 1)
+
+        def load_w2(e):
+            nc.sync.dma_start(out=w2_w[e][:].bitcast(I32), in_=w2_words[e, 0].bitcast(I32))
+
+        nc.sync.dma_start(offs_sb[:], offs)
+        nc.sync.dma_start(out=dy_w[:], in_=dy_words[0].rearrange("p n d -> p (n d)").bitcast(I32))
+        for r in range(4):
+            nc.sync.dma_start(out=dy_s[r:P:32, :].bitcast(I32), in_=dy_scales[0, r:16:4, :].bitcast(I32))
+        load_saved(0, 0)
+        load_w2(0)
+        for r in range(4):
+            nc.sync.dma_start(
+                out=w2_s[r:P:32, :, :].bitcast(I32),
+                in_=w2_scales[:, 0, r:16:4, :].rearrange("e q i -> q e i").bitcast(I32),
+            )
+        nc.sync.dma_start(out=gate_rows[0 : SLOTS // P, :], in_=gate[0].rearrange("(c p) -> c p", p=P))
+        load_saved(0, 1)
+        load_unit(1)
+        for m, (words, scales) in enumerate(((w1_words, w1_scales), (w3_words, w3_scales))):
+            for r in range(4):
+                nc.sync.dma_start(
+                    out=w13_s[m][r:P:32, :, :].bitcast(I32),
+                    in_=scales[:, :, r:16:4, :].rearrange("e s q k -> q (e s) k").bitcast(I32),
+                )
+        for m, (words, scales) in enumerate(((w1_words, w1_scales), (w3_words, w3_scales))):
+            nc.sync.dma_start(out=w13_w[m][:].bitcast(I32), in_=words.rearrange("e s p b -> p (e s) b").bitcast(I32))
+        load_unit(2)
+        for e in range(1, E):
+            load_w2(e)
+        nc.sync.dma_start(pos1_sb[:], pos1)
+        nc.sync.dma_start(pos2_sb[:], pos2)
+
+        def gather(e, lo, hi):
+            cols = slice((e * C + lo) // LIST_ROWS, (e * C + hi) // LIST_ROWS)
+            nc.vector.tensor_copy(g_w[e][:, lo:hi], dy_w[:].bitcast(U32).indirect(offs_sb[:, cols]))
+            nc.vector.tensor_copy(g_s[e][:, lo:hi], dy_s[:].indirect(offs_sb[:, cols]))
+
+        gate_bank = psum_dh.tile([P, PACK, P], F32, name="dh")
+        nc.tensor.transpose(gate_bank[:, 0, :], gate_rows[:], ident[:])
+        nc.scalar.activation(gate_col[:], gate_bank[:, 0, 0 : SLOTS // P], ACT.Copy)
+
+        gather(0, 0, P)
+        gather(0, P, C)
+
+        turned = {}
+        dh_banks = {}
+        factors = {}
+        da_tiles = {}
+        dx_banks = {}
+
+        def first_product(g):
+            u, j = divmod(g, CHUNKS)
+            e, h = divmod(u, HALVES)
+            slots = slice(j * P, (j + 1) * P)
+            bank = psum_first.tile([P, PASS], F32, name="first")
+            nc.tensor.matmul_mx(
+                out=bank[:],
+                lhsT=g_w[e][:, slots].bitcast(E5M2),
+                lhsT_scale=g_s[e][:, slots],
+                rhs=w2_w[e][:, 2 * h * PASS : 2 * (h + 1) * PASS].bitcast(E2M1),
+                rhs_scale=w2_s[:, e, h * PASS : (h + 1) * PASS],
+                start=True,
+                stop=True,
+            )
+            dh_t = work.tile([P, PACK, P], F32, name="dh_t")
+            c = e * CHUNKS + j
+            nc.scalar.activation(
+                dh_t[:], bank[:].rearrange("s (m t) -> s t m", t=PACK), ACT.Copy, scale=gate_col[:, c : c + 1]
+            )
+            turned[g] = dh_t
+
+        def turn(g):
+            bank = psum_dh.tile([P, PACK, P], F32, name="dh")
+            for t in range(PACK):
+                nc.tensor.transpose(bank[:, t, :], turned[g][:, t, :], ident[:])
+            dh_banks[g] = bank
+
+        def make_factors(g0, count):
+            u, j0 = divmod(g0, CHUNKS)
+            a1_sb, a3_sb = a_tiles[u, 0], a_tiles[u, 1]
+            s = pairs.tile([P, PACK, count * P], F32, name="s")
+            d = pairs.tile([P, PACK, count * P], F32, name="d")
+            nc.scalar.activation(s[:], a1_sb[:, :, j0 * P : (j0 + count) * P], ACT.Sigmoid)
+            nc.scalar.activation(d[:], s[:], ACT.Square, bias=minus_half[:])
+            for r in range(count):
+                g = g0 + r
+                own = slice(r * P, (r + 1) * P)
+                w = work.tile([P, PACK, P], F32, name="w")
+                if D_ENG[g] == "s":
+                    nc.scalar.activation(d[:, :, own], d[:, :, own], ACT.Copy, scale=-1.0, bias=0.25)
+                elif D_ENG[g] == "g":
+                    nc.gpsimd.tensor_scalar(d[:, :, own], d[:, :, own], -1.0, 0.25, ALU.mult, ALU.add)
+                else:
+                    nc.vector.tensor_scalar(d[:, :, own], d[:, :, own], -1.0, 0.25, ALU.mult, ALU.add)
+                engine = nc.gpsimd if W_ENG[g] == "g" else nc.vector
+                engine.tensor_tensor(w[:], d[:, :, own], a3_sb[:, :, (j0 + r) * P : (j0 + r + 1) * P], ALU.mult)
+                factors[g] = (w[:], s[:, :, own])
+
+        def products(g):
+            u, j = divmod(g, CHUNKS)
+            if j == 0:
+                da_tiles[u] = unit_pool.tile([P, 2, C, PACK], BF16, name="da", align_bytes=64)
+            bank = dh_banks[g][:].rearrange("p t (c i) -> p c t i", i=2)
+            for m in (1, 0):
+                nc.vector.tensor_tensor(
+                    da_tiles[u][:, m, j * P : (j + 1) * P, :].rearrange("p (c i) t -> p c t i", i=2),
+                    bank,
+                    factors[g][m].rearrange("p t (c i) -> p c t i", i=2),
+                    ALU.mult,
+                )
+
+        def second_product(u):
+            e, h = divmod(u, HALVES)
+            codes = unit_pool.tile([P, 2, C], U32, name="codes", align_bytes=64)
+            scales = unit_pool.tile([P, 2, C], U8, name="scales", align_bytes=64)
+            if u < UNITS - 1:
+                nc.vector.quantize_mx(
+                    out=codes[:].rearrange("p m n -> p (m n)").bitcast(E5M2),
+                    scales=scales[:].rearrange("p m n -> p (m n)"),
+                    in_=da_tiles[u][:].rearrange("p m n t -> p (m n t)"),
+                )
+            else:
+                for m in (1, 0):
+                    nc.vector.quantize_mx(
+                        out=codes[:, m, :].bitcast(E5M2),
+                        scales=scales[:, m, :],
+                        in_=da_tiles[u][:, m, :, :].rearrange("p n t -> p (n t)"),
+                    )
+            if h == 0:
+                dx_banks[e] = psum_dx.tile([K, C], F32, name="dx_bank")
+            for m in (1, 0):
+                nc.tensor.matmul_mx(
+                    out=dx_banks[e][:],
+                    lhsT=w13_w[m][:, u, :].bitcast(E2M1),
+                    lhsT_scale=w13_s[m][:, u, :],
+                    rhs=codes[:, m, :].bitcast(E5M2),
+                    rhs_scale=scales[:, m, :],
+                    start=(h == 0 and m == 1),
+                    stop=(h == HALVES - 1 and m == 0),
+                )
+            if h == HALVES - 1:
+                nc.scalar.activation(dx[:, e * C : (e + 1) * C], dx_banks[e][:], ACT.Copy)
+
+        total = UNITS * CHUNKS
+        make_factors(0, 1)
+        first_product(0)
+        make_factors(1, 1)
+        first_product(1)
+        turn(0)
+        make_factors(2, 2)
+        first_product(2)
+        turn(1)
+        for g in range(total):
+            u, j = divmod(g, CHUNKS)
+            if j == 0 and u + 3 < UNITS:
+                load_unit(u + 3)
+            if g + 3 < total:
+                first_product(g + 3)
+            if g + 2 < total:
+                turn(g + 2)
+            if g % 2 == 0 and g + 4 < total:
+                make_factors(g + 4, 2)
+            products(g)
+            if j == 0 and u > 0:
+                second_product(u - 1)
+            if j == 1 and u % HALVES == 0 and u // HALVES + 1 < E:
+                gather(u // HALVES + 1, 0, C)
+        second_product(UNITS - 1)
+
+        width = T // OUT_PIECES
+        for piece in range(OUT_PIECES):
+            cols = slice(piece * width // LIST_ROWS, (piece + 1) * width // LIST_ROWS)
+            first = work.tile([P, width], F32, name="first_slot")
+            second = work.tile([P, width], F32, name="second_slot")
+            nc.vector.tensor_copy(first[:], dx[:].indirect(pos1_sb[:, cols]))
+            nc.vector.tensor_copy(second[:], dx[:].indirect(pos2_sb[:, cols]))
+            nc.vector.tensor_tensor(first[:], first[:], second[:], ALU.add)
+            nc.sync.dma_start(out=out[:, piece * width : (piece + 1) * width], in_=first[:])

@@ -27,9 +27,10 @@ HALVES = H // PASS
 UNITS = E * HALVES
 CHUNKS = C // P
 LIST_ROWS = 16
-D_ENG = "gsgsgsgsgsgsgsgsgsgsgsgsgsgsgsgs"
-W_ENG = "gvgvgvgvgvgvgvgvgvgvgvgvgvgvgvgv"
-OUT_PIECES = 2
+SCALAR_COLS = 256
+STEP = 2
+STEPS = UNITS * CHUNKS // STEP
+OUT_PIECES = 4
 
 
 def tile_moe_bdx_glu_sigmoid_kernel(
@@ -39,9 +40,9 @@ def tile_moe_bdx_glu_sigmoid_kernel(
     nc = tc.nc
     with ExitStack() as ctx:
         keep = ctx.enter_context(tc.tile_pool(name="keep", bufs=1))
-        loads = ctx.enter_context(tc.tile_pool(name="loads", bufs=4))
-        work = ctx.enter_context(tc.tile_pool(name="work", bufs=6))
-        pairs = ctx.enter_context(tc.tile_pool(name="pairs", bufs=4))
+        loads = ctx.enter_context(tc.tile_pool(name="loads", bufs=3))
+        work = ctx.enter_context(tc.tile_pool(name="work", bufs=5))
+        pairs = ctx.enter_context(tc.tile_pool(name="pairs", bufs=5))
         unit_pool = ctx.enter_context(tc.tile_pool(name="unit", bufs=2))
         psum_first = ctx.enter_context(tc.psum_pool(name="psum_first", bufs=3))
         psum_dh = ctx.enter_context(tc.psum_pool(name="psum_dh", bufs=4))
@@ -74,44 +75,53 @@ def tile_moe_bdx_glu_sigmoid_kernel(
 
         a_tiles = {}
 
-        def load_saved(u, m):
+        def load_saved(u, m, first, count):
             e, h = divmod(u, HALVES)
-            tile = loads.tile([P, PACK, C], F32, name=("a1", "a3")[m])
-            rows = (a1, a3)[m][h * PASS : (h + 1) * PASS, e * C : (e + 1) * C]
+            tile = loads.tile([P, PACK, count * P], F32, name=("a1", "a3")[m] + ("", "_head")[count < CHUNKS])
+            lo = e * C + first * P
+            rows = (a1, a3)[m][h * PASS : (h + 1) * PASS, lo : lo + count * P]
             nc.sync.dma_start(out=tile[:], in_=rows.rearrange("(p t) n -> p t n", t=PACK))
-            a_tiles[u, m] = tile
+            for j in range(first, first + count):
+                a_tiles[u, m, j] = (tile, first)
 
-        def load_unit(u):
-            load_saved(u, 0)
-            load_saved(u, 1)
+        def saved(u, m, lo, hi):
+            tile, first = a_tiles[u, m, lo]
+            return tile[:, :, (lo - first) * P : (hi - first) * P].rearrange("p t (j n) -> p j t n", n=P)
 
         def load_w2(e):
             nc.sync.dma_start(out=w2_w[e][:].bitcast(I32), in_=w2_words[e, 0].bitcast(I32))
+
+        def load_w2_scales(r):
+            nc.sync.dma_start(
+                out=w2_s[r:P:32, :, :].bitcast(I32),
+                in_=w2_scales[:, 0, r:16:4, :].rearrange("e q i -> q e i").bitcast(I32),
+            )
 
         nc.sync.dma_start(offs_sb[:], offs)
         nc.sync.dma_start(out=dy_w[:], in_=dy_words[0].rearrange("p n d -> p (n d)").bitcast(I32))
         for r in range(4):
             nc.sync.dma_start(out=dy_s[r:P:32, :].bitcast(I32), in_=dy_scales[0, r:16:4, :].bitcast(I32))
-        load_saved(0, 0)
-        load_w2(0)
+        load_saved(0, 0, 0, 2)
         for r in range(4):
-            nc.sync.dma_start(
-                out=w2_s[r:P:32, :, :].bitcast(I32),
-                in_=w2_scales[:, 0, r:16:4, :].rearrange("e q i -> q e i").bitcast(I32),
-            )
+            load_w2_scales(r)
         nc.sync.dma_start(out=gate_rows[0 : SLOTS // P, :], in_=gate[0].rearrange("(c p) -> c p", p=P))
-        load_saved(0, 1)
-        load_unit(1)
+        load_w2(0)
+        load_saved(0, 1, 0, 2)
+        load_saved(0, 0, 2, 2)
+        load_saved(1, 0, 0, CHUNKS)
+        load_saved(0, 1, 2, 2)
+        load_w2(1)
         for m, (words, scales) in enumerate(((w1_words, w1_scales), (w3_words, w3_scales))):
             for r in range(4):
                 nc.sync.dma_start(
                     out=w13_s[m][r:P:32, :, :].bitcast(I32),
                     in_=scales[:, :, r:16:4, :].rearrange("e s q k -> q (e s) k").bitcast(I32),
                 )
+        load_saved(1, 1, 0, CHUNKS)
         for m, (words, scales) in enumerate(((w1_words, w1_scales), (w3_words, w3_scales))):
             nc.sync.dma_start(out=w13_w[m][:].bitcast(I32), in_=words.rearrange("e s p b -> p (e s) b").bitcast(I32))
-        load_unit(2)
-        for e in range(1, E):
+        load_saved(2, 0, 0, CHUNKS)
+        for e in range(2, E):
             load_w2(e)
         nc.sync.dma_start(pos1_sb[:], pos1)
         nc.sync.dma_start(pos2_sb[:], pos2)
@@ -121,16 +131,14 @@ def tile_moe_bdx_glu_sigmoid_kernel(
             nc.vector.tensor_copy(g_w[e][:, lo:hi], dy_w[:].bitcast(U32).indirect(offs_sb[:, cols]))
             nc.vector.tensor_copy(g_s[e][:, lo:hi], dy_s[:].indirect(offs_sb[:, cols]))
 
-        gate_bank = psum_dh.tile([P, PACK, P], F32, name="dh")
-        nc.tensor.transpose(gate_bank[:, 0, :], gate_rows[:], ident[:])
-        nc.scalar.activation(gate_col[:], gate_bank[:, 0, 0 : SLOTS // P], ACT.Copy)
-
         gather(0, 0, P)
         gather(0, P, C)
 
         turned = {}
         dh_banks = {}
-        factors = {}
+        s_tiles = {}
+        w_tiles = {}
+        code_tiles = {}
         da_tiles = {}
         dx_banks = {}
 
@@ -161,97 +169,123 @@ def tile_moe_bdx_glu_sigmoid_kernel(
                 nc.tensor.transpose(bank[:, t, :], turned[g][:, t, :], ident[:])
             dh_banks[g] = bank
 
-        def make_factors(g0, count):
-            u, j0 = divmod(g0, CHUNKS)
-            a1_sb, a3_sb = a_tiles[u, 0], a_tiles[u, 1]
-            s = pairs.tile([P, PACK, count * P], F32, name="s")
-            d = pairs.tile([P, PACK, count * P], F32, name="d")
-            nc.scalar.activation(s[:], a1_sb[:, :, j0 * P : (j0 + count) * P], ACT.Sigmoid)
-            nc.scalar.activation(d[:], s[:], ACT.Square, bias=minus_half[:])
-            for r in range(count):
-                g = g0 + r
-                own = slice(r * P, (r + 1) * P)
-                w = work.tile([P, PACK, P], F32, name="w")
-                if D_ENG[g] == "s":
-                    nc.scalar.activation(d[:, :, own], d[:, :, own], ACT.Copy, scale=-1.0, bias=0.25)
-                elif D_ENG[g] == "g":
-                    nc.gpsimd.tensor_scalar(d[:, :, own], d[:, :, own], -1.0, 0.25, ALU.mult, ALU.add)
-                else:
-                    nc.vector.tensor_scalar(d[:, :, own], d[:, :, own], -1.0, 0.25, ALU.mult, ALU.add)
-                engine = nc.gpsimd if W_ENG[g] == "g" else nc.vector
-                engine.tensor_tensor(w[:], d[:, :, own], a3_sb[:, :, (j0 + r) * P : (j0 + r + 1) * P], ALU.mult)
-                factors[g] = (w[:], s[:, :, own])
+        def saved_step(k, m):
+            u, lo = divmod(k * STEP, CHUNKS)
+            return saved(u, m, lo, lo + STEP)
 
-        def products(g):
+        def sigmoid_and_square(k):
+            s_tiles[k] = pairs.tile([P, STEP, PACK, P], F32, name="s")
+            w_tiles[k] = pairs.tile([P, STEP, PACK, P], F32, name="w")
+            nc.scalar.activation(s_tiles[k][:], saved_step(k, 0), ACT.Sigmoid)
+            nc.scalar.activation(w_tiles[k][:], s_tiles[k][:], ACT.Square, bias=minus_half[:])
+
+        def slope_scalar(k):
+            w = w_tiles[k][:].rearrange("p j t n -> p (j t n)")[:, 0:SCALAR_COLS]
+            nc.scalar.activation(w, w, ACT.Copy, scale=-1.0, bias=0.25)
+
+        def slope_vector_and_times_a3(k):
+            w = w_tiles[k][:].rearrange("p j t n -> p (j t n)")[:, SCALAR_COLS : STEP * PASS]
+            nc.vector.tensor_scalar(w, w, -1.0, 0.25, ALU.mult, ALU.add)
+            nc.gpsimd.tensor_tensor(w_tiles[k][:], w_tiles[k][:], saved_step(k, 1), ALU.mult)
+
+        def product(g, m):
             u, j = divmod(g, CHUNKS)
-            if j == 0:
+            if u not in da_tiles:
                 da_tiles[u] = unit_pool.tile([P, 2, C, PACK], BF16, name="da", align_bytes=64)
-            bank = dh_banks[g][:].rearrange("p t (c i) -> p c t i", i=2)
-            for m in (1, 0):
-                nc.vector.tensor_tensor(
-                    da_tiles[u][:, m, j * P : (j + 1) * P, :].rearrange("p (c i) t -> p c t i", i=2),
-                    bank,
-                    factors[g][m].rearrange("p t (c i) -> p c t i", i=2),
-                    ALU.mult,
+            factor = (w_tiles, s_tiles)[m][g // STEP][:, g % STEP, :, :]
+            nc.vector.tensor_tensor(
+                da_tiles[u][:, m, j * P : (j + 1) * P, :].rearrange("p (c i) t -> p c t i", i=2),
+                dh_banks[g][:].rearrange("p t (c i) -> p c t i", i=2),
+                factor.rearrange("p t (c i) -> p c t i", i=2),
+                ALU.mult,
+            )
+
+        def quantize(u, parts):
+            if u not in code_tiles:
+                codes = unit_pool.tile([P, 2 * C], U32, name="codes", align_bytes=64)
+                scales = unit_pool.tile([P, 2 * C], U8, name="scales", align_bytes=64)
+                code_tiles[u] = (codes, scales)
+            codes, scales = code_tiles[u]
+            values = da_tiles[u][:].rearrange("p m n t -> p (m n t)")
+            for lo, hi in parts:
+                nc.vector.quantize_mx(
+                    out=codes[:, lo:hi].bitcast(E5M2), scales=scales[:, lo:hi], in_=values[:, PACK * lo : PACK * hi]
                 )
 
-        def second_product(u):
+        def second_product(u, m):
             e, h = divmod(u, HALVES)
-            codes = unit_pool.tile([P, 2, C], U32, name="codes", align_bytes=64)
-            scales = unit_pool.tile([P, 2, C], U8, name="scales", align_bytes=64)
-            if u < UNITS - 1:
-                nc.vector.quantize_mx(
-                    out=codes[:].rearrange("p m n -> p (m n)").bitcast(E5M2),
-                    scales=scales[:].rearrange("p m n -> p (m n)"),
-                    in_=da_tiles[u][:].rearrange("p m n t -> p (m n t)"),
-                )
-            else:
-                for m in (1, 0):
-                    nc.vector.quantize_mx(
-                        out=codes[:, m, :].bitcast(E5M2),
-                        scales=scales[:, m, :],
-                        in_=da_tiles[u][:, m, :, :].rearrange("p n t -> p (n t)"),
-                    )
-            if h == 0:
+            codes, scales = code_tiles[u]
+            opens = h == 0 and m == 1
+            closes = h == HALVES - 1 and m == 0
+            if opens:
                 dx_banks[e] = psum_dx.tile([K, C], F32, name="dx_bank")
-            for m in (1, 0):
-                nc.tensor.matmul_mx(
-                    out=dx_banks[e][:],
-                    lhsT=w13_w[m][:, u, :].bitcast(E2M1),
-                    lhsT_scale=w13_s[m][:, u, :],
-                    rhs=codes[:, m, :].bitcast(E5M2),
-                    rhs_scale=scales[:, m, :],
-                    start=(h == 0 and m == 1),
-                    stop=(h == HALVES - 1 and m == 0),
-                )
-            if h == HALVES - 1:
+            nc.tensor.matmul_mx(
+                out=dx_banks[e][:],
+                lhsT=w13_w[m][:, u, :].bitcast(E2M1),
+                lhsT_scale=w13_s[m][:, u, :],
+                rhs=codes[:, m * C : (m + 1) * C].bitcast(E5M2),
+                rhs_scale=scales[:, m * C : (m + 1) * C],
+                start=opens,
+                stop=closes,
+            )
+            if closes:
                 nc.scalar.activation(dx[:, e * C : (e + 1) * C], dx_banks[e][:], ACT.Copy)
 
         total = UNITS * CHUNKS
-        make_factors(0, 1)
+        half = C // 2
+        sigmoid_and_square(0)
+        gate_bank = psum_dh.tile([P, PACK, P], F32, name="dh")
+        nc.tensor.transpose(gate_bank[:, 0, :], gate_rows[:], ident[:])
+        nc.scalar.activation(gate_col[:], gate_bank[:, 0, 0 : SLOTS // P], ACT.Copy)
+        slope_scalar(0)
         first_product(0)
-        make_factors(1, 1)
         first_product(1)
         turn(0)
-        make_factors(2, 2)
-        first_product(2)
         turn(1)
-        for g in range(total):
-            u, j = divmod(g, CHUNKS)
-            if j == 0 and u + 3 < UNITS:
-                load_unit(u + 3)
-            if g + 3 < total:
-                first_product(g + 3)
-            if g + 2 < total:
-                turn(g + 2)
-            if g % 2 == 0 and g + 4 < total:
-                make_factors(g + 4, 2)
-            products(g)
-            if j == 0 and u > 0:
-                second_product(u - 1)
-            if j == 1 and u % HALVES == 0 and u // HALVES + 1 < E:
-                gather(u // HALVES + 1, 0, C)
-        second_product(UNITS - 1)
+        gather(1, 0, C)
+        slope_vector_and_times_a3(0)
+        sigmoid_and_square(1)
+        slope_scalar(1)
+        product(0, 1)
+        product(1, 1)
+        for g in range(2, 6):
+            first_product(g)
+            if g < 4:
+                turn(g)
+        sigmoid_and_square(2)
+        for k in range(STEPS):
+            u = k // 2
+            if k % 2 == 0:
+                if u + 3 < UNITS:
+                    load_saved(u + 3, 0, 0, CHUNKS)
+                if u + 2 < UNITS:
+                    load_saved(u + 2, 1, 0, CHUNKS)
+                if u > 0:
+                    quantize(u - 1, [(0, 2 * C)])
+                    second_product(u - 1, 1)
+                    second_product(u - 1, 0)
+            elif u < 4:
+                gather(2 + u // 2, u % 2 * half, u % 2 * half + half)
+            if k + 1 < STEPS:
+                slope_vector_and_times_a3(k + 1)
+            else:
+                quantize(u, [(C, 2 * C), (0, half)])
+                second_product(u, 1)
+            if k + 2 < STEPS:
+                slope_scalar(k + 2)
+            for g in (2 * k, 2 * k + 1):
+                product(g, 0)
+                if g + 4 < total:
+                    turn(g + 4)
+                if g + 6 < total:
+                    first_product(g + 6)
+            if k + 3 < STEPS:
+                sigmoid_and_square(k + 3)
+            if k + 1 < STEPS:
+                product(2 * k + 2, 1)
+                product(2 * k + 3, 1)
+        quantize(UNITS - 1, [(half, C)])
+        second_product(UNITS - 1, 0)
 
         width = T // OUT_PIECES
         for piece in range(OUT_PIECES):

@@ -27,10 +27,9 @@ HALVES = H // PASS
 UNITS = E * HALVES
 CHUNKS = C // P
 LIST_ROWS = 16
-SCALAR_COLS = 256
 STEP = 2
 STEPS = UNITS * CHUNKS // STEP
-OUT_PIECES = 4
+OUT_PIECES = 2
 
 
 def tile_moe_bdx_glu_sigmoid_kernel(
@@ -57,8 +56,8 @@ def tile_moe_bdx_glu_sigmoid_kernel(
         w2_s = keep.tile([P, E, H], U8, name="w2_s", align_bytes=64)
         w13_w = [keep.tile([P, UNITS, 2 * K], U8, name="w13_w%d" % m, align_bytes=64) for m in range(2)]
         w13_s = [keep.tile([P, UNITS, K], U8, name="w13_s%d" % m, align_bytes=64) for m in range(2)]
-        g_w = [keep.tile([P, C], U32, name="g_w%d" % e, align_bytes=64) for e in range(E)]
-        g_s = [keep.tile([P, C], U8, name="g_s%d" % e, align_bytes=64) for e in range(E)]
+        g_w = keep.tile([P, SLOTS], U32, name="g_w", align_bytes=64)
+        g_s = keep.tile([P, SLOTS], U8, name="g_s", align_bytes=64)
         ident = keep.tile([P, P], F32, name="ident")
         gate_rows = keep.tile([P, P], F32, name="gate_rows")
         gate_col = keep.tile([P, SLOTS // P], F32, name="gate_col")
@@ -126,18 +125,23 @@ def tile_moe_bdx_glu_sigmoid_kernel(
         nc.sync.dma_start(pos1_sb[:], pos1)
         nc.sync.dma_start(pos2_sb[:], pos2)
 
-        def gather(e, lo, hi):
-            cols = slice((e * C + lo) // LIST_ROWS, (e * C + hi) // LIST_ROWS)
-            nc.vector.tensor_copy(g_w[e][:, lo:hi], dy_w[:].bitcast(U32).indirect(offs_sb[:, cols]))
-            nc.vector.tensor_copy(g_s[e][:, lo:hi], dy_s[:].indirect(offs_sb[:, cols]))
+        def gather_words(lo, hi):
+            cols = slice(lo // LIST_ROWS, hi // LIST_ROWS)
+            nc.vector.tensor_copy(g_w[:, lo:hi], dy_w[:].bitcast(U32).indirect(offs_sb[:, cols]))
 
-        gather(0, 0, P)
-        gather(0, P, C)
+        def gather_scales(lo, hi):
+            cols = slice(lo // LIST_ROWS, hi // LIST_ROWS)
+            nc.vector.tensor_copy(g_s[:, lo:hi], dy_s[:].indirect(offs_sb[:, cols]))
+
+        cuts = (0, C, C + 3 * T // 4, SLOTS)
+        gather_words(cuts[0], cuts[1])
+        gather_scales(cuts[0], cuts[1])
 
         turned = {}
         dh_banks = {}
         s_tiles = {}
         w_tiles = {}
+        q_tiles = {}
         code_tiles = {}
         da_tiles = {}
         dx_banks = {}
@@ -145,12 +149,12 @@ def tile_moe_bdx_glu_sigmoid_kernel(
         def first_product(g):
             u, j = divmod(g, CHUNKS)
             e, h = divmod(u, HALVES)
-            slots = slice(j * P, (j + 1) * P)
+            slots = slice(e * C + j * P, e * C + (j + 1) * P)
             bank = psum_first.tile([P, PASS], F32, name="first")
             nc.tensor.matmul_mx(
                 out=bank[:],
-                lhsT=g_w[e][:, slots].bitcast(E5M2),
-                lhsT_scale=g_s[e][:, slots],
+                lhsT=g_w[:, slots].bitcast(E5M2),
+                lhsT_scale=g_s[:, slots],
                 rhs=w2_w[e][:, 2 * h * PASS : 2 * (h + 1) * PASS].bitcast(E2M1),
                 rhs_scale=w2_s[:, e, h * PASS : (h + 1) * PASS],
                 start=True,
@@ -159,7 +163,10 @@ def tile_moe_bdx_glu_sigmoid_kernel(
             dh_t = work.tile([P, PACK, P], F32, name="dh_t")
             c = e * CHUNKS + j
             nc.scalar.activation(
-                dh_t[:], bank[:].rearrange("s (m t) -> s t m", t=PACK), ACT.Copy, scale=gate_col[:, c : c + 1]
+                dh_t[:].rearrange("s t (r i) -> s r t i", i=2),
+                bank[:].rearrange("s (r i t) -> s r t i", i=2, t=PACK),
+                ACT.Copy,
+                scale=gate_col[:, c : c + 1],
             )
             turned[g] = dh_t
 
@@ -175,17 +182,13 @@ def tile_moe_bdx_glu_sigmoid_kernel(
 
         def sigmoid_and_square(k):
             s_tiles[k] = pairs.tile([P, STEP, PACK, P], F32, name="s")
-            w_tiles[k] = pairs.tile([P, STEP, PACK, P], F32, name="w")
+            q_tiles[k] = pairs.tile([P, STEP, PACK, P], F32, name="q")
             nc.scalar.activation(s_tiles[k][:], saved_step(k, 0), ACT.Sigmoid)
-            nc.scalar.activation(w_tiles[k][:], s_tiles[k][:], ACT.Square, bias=minus_half[:])
-
-        def slope_scalar(k):
-            w = w_tiles[k][:].rearrange("p j t n -> p (j t n)")[:, 0:SCALAR_COLS]
-            nc.scalar.activation(w, w, ACT.Copy, scale=-1.0, bias=0.25)
+            nc.scalar.activation(q_tiles[k][:], s_tiles[k][:], ACT.Square, bias=minus_half[:])
 
         def slope_vector_and_times_a3(k):
-            w = w_tiles[k][:].rearrange("p j t n -> p (j t n)")[:, SCALAR_COLS : STEP * PASS]
-            nc.vector.tensor_scalar(w, w, -1.0, 0.25, ALU.mult, ALU.add)
+            w_tiles[k] = unit_pool.tile([P, STEP, PACK, P], F32, name="w")
+            nc.vector.tensor_scalar(w_tiles[k][:], q_tiles[k][:], -1.0, 0.25, ALU.mult, ALU.add)
             nc.gpsimd.tensor_tensor(w_tiles[k][:], w_tiles[k][:], saved_step(k, 1), ALU.mult)
 
         def product(g, m):
@@ -237,17 +240,18 @@ def tile_moe_bdx_glu_sigmoid_kernel(
         gate_bank = psum_dh.tile([P, PACK, P], F32, name="dh")
         nc.tensor.transpose(gate_bank[:, 0, :], gate_rows[:], ident[:])
         nc.scalar.activation(gate_col[:], gate_bank[:, 0, 0 : SLOTS // P], ACT.Copy)
-        slope_scalar(0)
         first_product(0)
         first_product(1)
         turn(0)
         turn(1)
-        gather(1, 0, C)
+        gather_words(cuts[1], cuts[2])
+        gather_scales(cuts[1], cuts[2])
+        gather_words(cuts[2], cuts[3])
         slope_vector_and_times_a3(0)
         sigmoid_and_square(1)
-        slope_scalar(1)
         product(0, 1)
         product(1, 1)
+        gather_scales(cuts[2], cuts[3])
         for g in range(2, 6):
             first_product(g)
             if g < 4:
@@ -264,15 +268,11 @@ def tile_moe_bdx_glu_sigmoid_kernel(
                     quantize(u - 1, [(0, 2 * C)])
                     second_product(u - 1, 1)
                     second_product(u - 1, 0)
-            elif u < 4:
-                gather(2 + u // 2, u % 2 * half, u % 2 * half + half)
             if k + 1 < STEPS:
                 slope_vector_and_times_a3(k + 1)
             else:
                 quantize(u, [(C, 2 * C), (0, half)])
                 second_product(u, 1)
-            if k + 2 < STEPS:
-                slope_scalar(k + 2)
             for g in (2 * k, 2 * k + 1):
                 product(g, 0)
                 if g + 4 < total:
@@ -288,11 +288,18 @@ def tile_moe_bdx_glu_sigmoid_kernel(
         second_product(UNITS - 1, 0)
 
         width = T // OUT_PIECES
-        for piece in range(OUT_PIECES):
+        fetched = {}
+
+        def fetch(piece, m):
             cols = slice(piece * width // LIST_ROWS, (piece + 1) * width // LIST_ROWS)
-            first = work.tile([P, width], F32, name="first_slot")
-            second = work.tile([P, width], F32, name="second_slot")
-            nc.vector.tensor_copy(first[:], dx[:].indirect(pos1_sb[:, cols]))
-            nc.vector.tensor_copy(second[:], dx[:].indirect(pos2_sb[:, cols]))
-            nc.vector.tensor_tensor(first[:], first[:], second[:], ALU.add)
-            nc.sync.dma_start(out=out[:, piece * width : (piece + 1) * width], in_=first[:])
+            fetched[piece, m] = work.tile([P, width], F32, name=("first_slot", "second_slot")[m])
+            nc.vector.tensor_copy(fetched[piece, m][:], dx[:].indirect((pos1_sb, pos2_sb)[m][:, cols]))
+
+        fetch(0, 0)
+        for piece in range(OUT_PIECES):
+            fetch(piece, 1)
+            if piece + 1 < OUT_PIECES:
+                fetch(piece + 1, 0)
+            both = fetched[piece, 0]
+            nc.vector.tensor_tensor(both[:], both[:], fetched[piece, 1][:], ALU.add)
+            nc.sync.dma_start(out=out[:, piece * width : (piece + 1) * width], in_=both[:])

@@ -41,7 +41,8 @@ def tile_moe_bdx_glu_sigmoid_kernel(
         keep = ctx.enter_context(tc.tile_pool(name="keep", bufs=1))
         loads = ctx.enter_context(tc.tile_pool(name="loads", bufs=3))
         work = ctx.enter_context(tc.tile_pool(name="work", bufs=5))
-        pairs = ctx.enter_context(tc.tile_pool(name="pairs", bufs=5))
+        pairs = ctx.enter_context(tc.tile_pool(name="pairs", bufs=4))
+        single = ctx.enter_context(tc.tile_pool(name="single", bufs=1))
         unit_pool = ctx.enter_context(tc.tile_pool(name="unit", bufs=2))
         psum_first = ctx.enter_context(tc.psum_pool(name="psum_first", bufs=3))
         psum_dh = ctx.enter_context(tc.psum_pool(name="psum_dh", bufs=4))
@@ -61,13 +62,11 @@ def tile_moe_bdx_glu_sigmoid_kernel(
         ident = keep.tile([P, P], F32, name="ident")
         gate_rows = keep.tile([P, P], F32, name="gate_rows")
         gate_col = keep.tile([P, SLOTS // P], F32, name="gate_col")
-        minus_half = keep.tile([P, 1], F32, name="minus_half")
         dx = keep.tile([P, SLOTS], F32, name="dx")
 
         nc.vector.memset(dy_s[:].bitcast(I32), 0)
         nc.vector.memset(w2_s[:].rearrange("p e i -> p (e i)").bitcast(I32), 0)
         nc.vector.memset(gate_rows[:], 0.0)
-        nc.vector.memset(minus_half[:], -0.5)
         for m in range(2):
             nc.vector.memset(w13_s[m][:].rearrange("p u k -> p (u k)").bitcast(I32), 0)
         make_identity(nc, ident[:])
@@ -141,7 +140,7 @@ def tile_moe_bdx_glu_sigmoid_kernel(
         dh_banks = {}
         s_tiles = {}
         w_tiles = {}
-        q_tiles = {}
+        da3_tiles = {}
         code_tiles = {}
         da_tiles = {}
         dx_banks = {}
@@ -180,26 +179,47 @@ def tile_moe_bdx_glu_sigmoid_kernel(
             u, lo = divmod(k * STEP, CHUNKS)
             return saved(u, m, lo, lo + STEP)
 
-        def sigmoid_and_square(k):
+        def sigmoid(k):
             s_tiles[k] = pairs.tile([P, STEP, PACK, P], F32, name="s")
-            q_tiles[k] = pairs.tile([P, STEP, PACK, P], F32, name="q")
-            nc.scalar.activation(s_tiles[k][:], saved_step(k, 0), ACT.Sigmoid)
-            nc.scalar.activation(q_tiles[k][:], s_tiles[k][:], ACT.Square, bias=minus_half[:])
+            nc.scalar.activation(s_tiles[k][:], saved_step(k, 0), ACT.Sigmoid, scale=-1.0)
 
-        def slope_vector_and_times_a3(k):
-            w_tiles[k] = unit_pool.tile([P, STEP, PACK, P], F32, name="w")
-            nc.vector.tensor_scalar(w_tiles[k][:], q_tiles[k][:], -1.0, 0.25, ALU.mult, ALU.add)
-            nc.gpsimd.tensor_tensor(w_tiles[k][:], w_tiles[k][:], saved_step(k, 1), ALU.mult)
+        def times_a3(g):
+            u, j = divmod(g, CHUNKS)
+            pool, engine = ((single, nc.gpsimd), (unit_pool, nc.vector))[g % STEP]
+            w_tiles[g] = pool.tile([P, PACK, P], F32, name="w")
+            a3_sb = saved(u, 1, j, j + 1)[:, 0, :, :]
+            engine.tensor_tensor(w_tiles[g][:], s_tiles[g // STEP][:, g % STEP, :, :], a3_sb, ALU.mult)
 
-        def product(g, m):
+        def make_da3(g):
+            k, r = divmod(g, STEP)
+            if r == 0:
+                da3_tiles[k] = pairs.tile([P, PACK, STEP * P], F32, name="da3")
+            nc.vector.scalar_tensor_tensor(
+                da3_tiles[k][:, :, r * P : (r + 1) * P],
+                s_tiles[k][:, r, :, :],
+                1.0,
+                dh_banks[g][:],
+                ALU.subtract,
+                ALU.mult,
+            )
+
+        def packed(g, m, count):
             u, j = divmod(g, CHUNKS)
             if u not in da_tiles:
                 da_tiles[u] = unit_pool.tile([P, 2, C, PACK], BF16, name="da", align_bytes=64)
-            factor = (w_tiles, s_tiles)[m][g // STEP][:, g % STEP, :, :]
+            return da_tiles[u][:, m, j * P : (j + count) * P, :].rearrange("p (c i) t -> p c t i", i=2)
+
+        def round_da3(k):
+            nc.scalar.activation(
+                packed(k * STEP, 1, STEP), da3_tiles[k][:].rearrange("p t (c i) -> p c t i", i=2), ACT.Copy
+            )
+
+        def make_da1(g):
+            k, r = divmod(g, STEP)
             nc.vector.tensor_tensor(
-                da_tiles[u][:, m, j * P : (j + 1) * P, :].rearrange("p (c i) t -> p c t i", i=2),
-                dh_banks[g][:].rearrange("p t (c i) -> p c t i", i=2),
-                factor.rearrange("p t (c i) -> p c t i", i=2),
+                packed(g, 0, 1),
+                da3_tiles[k][:, :, r * P : (r + 1) * P].rearrange("p t (c i) -> p c t i", i=2),
+                w_tiles[g][:].rearrange("p t (c i) -> p c t i", i=2),
                 ALU.mult,
             )
 
@@ -236,27 +256,20 @@ def tile_moe_bdx_glu_sigmoid_kernel(
 
         total = UNITS * CHUNKS
         half = C // 2
-        sigmoid_and_square(0)
+        sigmoid(0)
         gate_bank = psum_dh.tile([P, PACK, P], F32, name="dh")
         nc.tensor.transpose(gate_bank[:, 0, :], gate_rows[:], ident[:])
-        nc.scalar.activation(gate_col[:], gate_bank[:, 0, 0 : SLOTS // P], ACT.Copy)
-        first_product(0)
-        first_product(1)
-        turn(0)
-        turn(1)
-        gather_words(cuts[1], cuts[2])
-        gather_scales(cuts[1], cuts[2])
-        gather_words(cuts[2], cuts[3])
-        slope_vector_and_times_a3(0)
-        sigmoid_and_square(1)
-        product(0, 1)
-        product(1, 1)
-        gather_scales(cuts[2], cuts[3])
-        for g in range(2, 6):
+        nc.scalar.activation(gate_col[:], gate_bank[:, 0, 0 : SLOTS // P], ACT.Copy, scale=-1.0)
+        for lo, hi in zip(cuts[1:-1], cuts[2:]):
+            gather_words(lo, hi)
+            gather_scales(lo, hi)
+        times_a3(1)
+        for g in range(6):
             first_product(g)
             if g < 4:
                 turn(g)
-        sigmoid_and_square(2)
+            if g in (1, 3):
+                sigmoid(g // 2 + 1)
         for k in range(STEPS):
             u = k // 2
             if k % 2 == 0:
@@ -264,26 +277,29 @@ def tile_moe_bdx_glu_sigmoid_kernel(
                     load_saved(u + 3, 0, 0, CHUNKS)
                 if u + 2 < UNITS:
                     load_saved(u + 2, 1, 0, CHUNKS)
-                if u > 0:
-                    quantize(u - 1, [(0, 2 * C)])
-                    second_product(u - 1, 1)
-                    second_product(u - 1, 0)
-            if k + 1 < STEPS:
-                slope_vector_and_times_a3(k + 1)
-            else:
-                quantize(u, [(C, 2 * C), (0, half)])
-                second_product(u, 1)
+            times_a3(2 * k)
             for g in (2 * k, 2 * k + 1):
-                product(g, 0)
+                make_da3(g)
                 if g + 4 < total:
                     turn(g + 4)
+            round_da3(k)
+            for g in (2 * k, 2 * k + 1):
                 if g + 6 < total:
                     first_product(g + 6)
             if k + 3 < STEPS:
-                sigmoid_and_square(k + 3)
+                sigmoid(k + 3)
             if k + 1 < STEPS:
-                product(2 * k + 2, 1)
-                product(2 * k + 3, 1)
+                times_a3(2 * k + 3)
+            else:
+                quantize(u, [(C, C + half), (0, half)])
+            if k % 2 == 0 and u > 0:
+                quantize(u - 1, [(0, 2 * C)])
+                second_product(u - 1, 1)
+                second_product(u - 1, 0)
+            make_da1(2 * k)
+            make_da1(2 * k + 1)
+        quantize(UNITS - 1, [(C + half, 2 * C)])
+        second_product(UNITS - 1, 1)
         quantize(UNITS - 1, [(half, C)])
         second_product(UNITS - 1, 0)
 

@@ -27,9 +27,6 @@ HALVES = H // PASS
 UNITS = E * HALVES
 CHUNKS = C // P
 LIST_ROWS = 16
-STEP = 2
-STEPS = UNITS * CHUNKS // STEP
-OUT_PIECES = 2
 
 
 def tile_moe_bdx_glu_sigmoid_kernel(
@@ -40,8 +37,8 @@ def tile_moe_bdx_glu_sigmoid_kernel(
     with ExitStack() as ctx:
         keep = ctx.enter_context(tc.tile_pool(name="keep", bufs=1))
         loads = ctx.enter_context(tc.tile_pool(name="loads", bufs=3))
-        work = ctx.enter_context(tc.tile_pool(name="work", bufs=5))
-        pairs = ctx.enter_context(tc.tile_pool(name="pairs", bufs=4))
+        work = ctx.enter_context(tc.tile_pool(name="work", bufs=8))
+        pairs = ctx.enter_context(tc.tile_pool(name="pairs", bufs=3))
         single = ctx.enter_context(tc.tile_pool(name="single", bufs=1))
         unit_pool = ctx.enter_context(tc.tile_pool(name="unit", bufs=2))
         psum_first = ctx.enter_context(tc.psum_pool(name="psum_first", bufs=3))
@@ -73,18 +70,11 @@ def tile_moe_bdx_glu_sigmoid_kernel(
 
         a_tiles = {}
 
-        def load_saved(u, m, first, count):
+        def load_saved(u, m):
             e, h = divmod(u, HALVES)
-            tile = loads.tile([P, PACK, count * P], F32, name=("a1", "a3")[m] + ("", "_head")[count < CHUNKS])
-            lo = e * C + first * P
-            rows = (a1, a3)[m][h * PASS : (h + 1) * PASS, lo : lo + count * P]
-            nc.sync.dma_start(out=tile[:], in_=rows.rearrange("(p t) n -> p t n", t=PACK))
-            for j in range(first, first + count):
-                a_tiles[u, m, j] = (tile, first)
-
-        def saved(u, m, lo, hi):
-            tile, first = a_tiles[u, m, lo]
-            return tile[:, :, (lo - first) * P : (hi - first) * P].rearrange("p t (j n) -> p j t n", n=P)
+            a_tiles[u, m] = loads.tile([P, PACK, C], F32, name=("a1", "a3")[m])
+            rows = (a1, a3)[m][h * PASS : (h + 1) * PASS, e * C : (e + 1) * C]
+            nc.sync.dma_start(out=a_tiles[u, m][:], in_=rows.rearrange("(p t) n -> p t n", t=PACK))
 
         def load_w2(e):
             nc.sync.dma_start(out=w2_w[e][:].bitcast(I32), in_=w2_words[e, 0].bitcast(I32))
@@ -97,17 +87,15 @@ def tile_moe_bdx_glu_sigmoid_kernel(
 
         nc.sync.dma_start(offs_sb[:], offs)
         nc.sync.dma_start(out=dy_w[:], in_=dy_words[0].rearrange("p n d -> p (n d)").bitcast(I32))
+        load_saved(0, 0)
         for r in range(4):
             nc.sync.dma_start(out=dy_s[r:P:32, :].bitcast(I32), in_=dy_scales[0, r:16:4, :].bitcast(I32))
-        load_saved(0, 0, 0, 2)
+        nc.sync.dma_start(out=gate_rows[0 : SLOTS // P, :], in_=gate[0].rearrange("(c p) -> c p", p=P))
         for r in range(4):
             load_w2_scales(r)
-        nc.sync.dma_start(out=gate_rows[0 : SLOTS // P, :], in_=gate[0].rearrange("(c p) -> c p", p=P))
         load_w2(0)
-        load_saved(0, 1, 0, 2)
-        load_saved(0, 0, 2, 2)
-        load_saved(1, 0, 0, CHUNKS)
-        load_saved(0, 1, 2, 2)
+        load_saved(1, 0)
+        load_saved(0, 1)
         load_w2(1)
         for m, (words, scales) in enumerate(((w1_words, w1_scales), (w3_words, w3_scales))):
             for r in range(4):
@@ -115,10 +103,10 @@ def tile_moe_bdx_glu_sigmoid_kernel(
                     out=w13_s[m][r:P:32, :, :].bitcast(I32),
                     in_=scales[:, :, r:16:4, :].rearrange("e s q k -> q (e s) k").bitcast(I32),
                 )
-        load_saved(1, 1, 0, CHUNKS)
+        load_saved(1, 1)
         for m, (words, scales) in enumerate(((w1_words, w1_scales), (w3_words, w3_scales))):
             nc.sync.dma_start(out=w13_w[m][:].bitcast(I32), in_=words.rearrange("e s p b -> p (e s) b").bitcast(I32))
-        load_saved(2, 0, 0, CHUNKS)
+        load_saved(2, 0)
         for e in range(2, E):
             load_w2(e)
         nc.sync.dma_start(pos1_sb[:], pos1)
@@ -136,6 +124,7 @@ def tile_moe_bdx_glu_sigmoid_kernel(
         gather_words(cuts[0], cuts[1])
         gather_scales(cuts[0], cuts[1])
 
+        half = C // 2
         turned = {}
         dh_banks = {}
         s_tiles = {}
@@ -175,51 +164,40 @@ def tile_moe_bdx_glu_sigmoid_kernel(
                 nc.tensor.transpose(bank[:, t, :], turned[g][:, t, :], ident[:])
             dh_banks[g] = bank
 
-        def saved_step(k, m):
-            u, lo = divmod(k * STEP, CHUNKS)
-            return saved(u, m, lo, lo + STEP)
+        def sigmoid(u):
+            s_tiles[u] = pairs.tile([P, PACK, C], F32, name="s")
+            nc.scalar.activation(s_tiles[u][:], a_tiles[u, 0][:], ACT.Sigmoid, scale=-1.0)
 
-        def sigmoid(k):
-            s_tiles[k] = pairs.tile([P, STEP, PACK, P], F32, name="s")
-            nc.scalar.activation(s_tiles[k][:], saved_step(k, 0), ACT.Sigmoid, scale=-1.0)
-
-        def times_a3(g):
-            u, j = divmod(g, CHUNKS)
-            pool, engine = ((single, nc.gpsimd), (unit_pool, nc.vector))[g % STEP]
-            w_tiles[g] = pool.tile([P, PACK, P], F32, name="w")
-            a3_sb = saved(u, 1, j, j + 1)[:, 0, :, :]
-            engine.tensor_tensor(w_tiles[g][:], s_tiles[g // STEP][:, g % STEP, :, :], a3_sb, ALU.mult)
+        def times_a3(u, part):
+            pool = (single, unit_pool)[part]
+            engine = nc.gpsimd if part == 0 or u == 0 else nc.vector
+            w_tiles[u, part] = pool.tile([P, PACK, half], F32, name="w")
+            cols = slice(part * half, (part + 1) * half)
+            engine.tensor_tensor(w_tiles[u, part][:], s_tiles[u][:, :, cols], a_tiles[u, 1][:, :, cols], ALU.mult)
 
         def make_da3(g):
-            k, r = divmod(g, STEP)
-            if r == 0:
-                da3_tiles[k] = pairs.tile([P, PACK, STEP * P], F32, name="da3")
-            nc.vector.scalar_tensor_tensor(
-                da3_tiles[k][:, :, r * P : (r + 1) * P],
-                s_tiles[k][:, r, :, :],
-                1.0,
-                dh_banks[g][:],
-                ALU.subtract,
-                ALU.mult,
-            )
-
-        def packed(g, m, count):
             u, j = divmod(g, CHUNKS)
-            if u not in da_tiles:
+            if j == 0:
+                da3_tiles[u] = unit_pool.tile([P, PACK, C], F32, name="da3")
                 da_tiles[u] = unit_pool.tile([P, 2, C, PACK], BF16, name="da", align_bytes=64)
-            return da_tiles[u][:, m, j * P : (j + count) * P, :].rearrange("p (c i) t -> p c t i", i=2)
-
-        def round_da3(k):
-            nc.scalar.activation(
-                packed(k * STEP, 1, STEP), da3_tiles[k][:].rearrange("p t (c i) -> p c t i", i=2), ACT.Copy
+            cols = slice(j * P, (j + 1) * P)
+            nc.vector.scalar_tensor_tensor(
+                da3_tiles[u][:, :, cols], s_tiles[u][:, :, cols], 1.0, dh_banks[g][:], ALU.subtract, ALU.mult
             )
 
-        def make_da1(g):
-            k, r = divmod(g, STEP)
+        def round_da3(u, lo, hi):
+            nc.scalar.activation(
+                da_tiles[u][:, 1, lo:hi, :].rearrange("p (c i) t -> p c t i", i=2),
+                da3_tiles[u][:, :, lo:hi].rearrange("p t (c i) -> p c t i", i=2),
+                ACT.Copy,
+            )
+
+        def make_da1(u, part):
+            cols = slice(part * half, (part + 1) * half)
             nc.vector.tensor_tensor(
-                packed(g, 0, 1),
-                da3_tiles[k][:, :, r * P : (r + 1) * P].rearrange("p t (c i) -> p c t i", i=2),
-                w_tiles[g][:].rearrange("p t (c i) -> p c t i", i=2),
+                da_tiles[u][:, 0, cols, :].rearrange("p (c i) t -> p c t i", i=2),
+                da3_tiles[u][:, :, cols].rearrange("p t (c i) -> p c t i", i=2),
+                w_tiles[u, part][:].rearrange("p t (c i) -> p c t i", i=2),
                 ALU.mult,
             )
 
@@ -255,7 +233,7 @@ def tile_moe_bdx_glu_sigmoid_kernel(
                 nc.scalar.activation(dx[:, e * C : (e + 1) * C], dx_banks[e][:], ACT.Copy)
 
         total = UNITS * CHUNKS
-        half = C // 2
+        last = UNITS - 1
         sigmoid(0)
         gate_bank = psum_dh.tile([P, PACK, P], F32, name="dh")
         nc.tensor.transpose(gate_bank[:, 0, :], gate_rows[:], ident[:])
@@ -263,59 +241,64 @@ def tile_moe_bdx_glu_sigmoid_kernel(
         for lo, hi in zip(cuts[1:-1], cuts[2:]):
             gather_words(lo, hi)
             gather_scales(lo, hi)
-        times_a3(1)
-        for g in range(6):
+        for g in range(CHUNKS):
             first_product(g)
-            if g < 4:
-                turn(g)
-            if g in (1, 3):
-                sigmoid(g // 2 + 1)
-        for k in range(STEPS):
-            u = k // 2
-            if k % 2 == 0:
-                if u + 3 < UNITS:
-                    load_saved(u + 3, 0, 0, CHUNKS)
-                if u + 2 < UNITS:
-                    load_saved(u + 2, 1, 0, CHUNKS)
-            times_a3(2 * k)
-            for g in (2 * k, 2 * k + 1):
+            turn(g)
+        sigmoid(1)
+        for g in range(CHUNKS, 2 * CHUNKS):
+            first_product(g)
+        for u in range(UNITS):
+            if u + 3 < UNITS:
+                load_saved(u + 3, 0)
+            if u + 2 < UNITS:
+                load_saved(u + 2, 1)
+            times_a3(u, 0)
+            if u == 0:
+                times_a3(u, 1)
+            for g in range(u * CHUNKS, (u + 1) * CHUNKS):
                 make_da3(g)
-                if g + 4 < total:
-                    turn(g + 4)
-            round_da3(k)
-            for g in (2 * k, 2 * k + 1):
-                if g + 6 < total:
-                    first_product(g + 6)
-            if k + 3 < STEPS:
-                sigmoid(k + 3)
-            if k + 1 < STEPS:
-                times_a3(2 * k + 3)
-            else:
-                quantize(u, [(C, C + half), (0, half)])
-            if k % 2 == 0 and u > 0:
+                if g + CHUNKS < total:
+                    turn(g + CHUNKS)
+                if u == last and g % 2 == 1:
+                    round_da3(u, g % CHUNKS // 2 * half, (g % CHUNKS // 2 + 1) * half)
+            if u + 2 < UNITS:
+                sigmoid(u + 2)
+            if u < last:
+                round_da3(u, 0, C)
+            for g in range((u + 2) * CHUNKS, min(total, (u + 3) * CHUNKS)):
+                first_product(g)
+            if u < last:
+                times_a3(u + 1, 1)
+            if u > 0:
                 quantize(u - 1, [(0, 2 * C)])
                 second_product(u - 1, 1)
                 second_product(u - 1, 0)
-            make_da1(2 * k)
-            make_da1(2 * k + 1)
-        quantize(UNITS - 1, [(C + half, 2 * C)])
-        second_product(UNITS - 1, 1)
-        quantize(UNITS - 1, [(half, C)])
-        second_product(UNITS - 1, 0)
+            make_da1(u, 0)
+            if u == last:
+                quantize(u, [(C, 2 * C)])
+                second_product(u, 1)
+            make_da1(u, 1)
+        quantize(last, [(0, half), (half, C)])
+        second_product(last, 0)
 
-        width = T // OUT_PIECES
+        pieces = ((0, T // 2), (T // 2, T))
         fetched = {}
 
         def fetch(piece, m):
-            cols = slice(piece * width // LIST_ROWS, (piece + 1) * width // LIST_ROWS)
-            fetched[piece, m] = work.tile([P, width], F32, name=("first_slot", "second_slot")[m])
-            nc.vector.tensor_copy(fetched[piece, m][:], dx[:].indirect((pos1_sb, pos2_sb)[m][:, cols]))
+            lo, hi = pieces[piece]
+            fetched[piece, m] = unit_pool.tile([P, hi - lo], F32, name=("first_slot", "second_slot")[m])
+            offsets = (pos1_sb, pos2_sb)[m][:, lo // LIST_ROWS : hi // LIST_ROWS]
+            nc.vector.tensor_copy(fetched[piece, m][:], dx[:].indirect(offsets))
 
-        fetch(0, 0)
-        for piece in range(OUT_PIECES):
-            fetch(piece, 1)
-            if piece + 1 < OUT_PIECES:
-                fetch(piece + 1, 0)
+        def add_and_store(piece):
+            lo, hi = pieces[piece]
             both = fetched[piece, 0]
             nc.vector.tensor_tensor(both[:], both[:], fetched[piece, 1][:], ALU.add)
-            nc.sync.dma_start(out=out[:, piece * width : (piece + 1) * width], in_=both[:])
+            nc.sync.dma_start(out=out[:, lo:hi], in_=both[:])
+
+        fetch(0, 0)
+        fetch(0, 1)
+        fetch(1, 0)
+        add_and_store(0)
+        fetch(1, 1)
+        add_and_store(1)

from contextlib import ExitStack

import concourse.mybir as mybir
from concourse.masks import make_identity

K, T, E, C, H, N = 128, 1024, 4, 512, 1024, 512
SLOTS = E * C
FLOPS = 2 * SLOTS * H * (N + 2 * K)
BYTES = (N * T + N * T // 32 + 2 * 4 * H * SLOTS + E * H * (N + 2 * K) // 2 + E * H * (N + 2 * K) // 32
         + 4 * SLOTS + 2 * 8 * (SLOTS + 2 * T) + 4 * K * T)

F32 = mybir.dt.float32
BF16 = mybir.dt.bfloat16
I32 = mybir.dt.int32
U32 = mybir.dt.uint32
U16 = mybir.dt.uint16
U8 = mybir.dt.uint8
E5M2 = mybir.dt.float8_e5m2_x4
E2M1 = mybir.dt.float4_e2m1fn_x4
ACT = mybir.ActivationFunctionType
ALU = mybir.AluOpType

P = 128
PACK = 4
PASS = P * PACK
HALVES = H // PASS
UNITS = E * HALVES
CHUNKS = C // P
LIST_ROWS = 16


def tile_moe_bdx_glu_sigmoid_kernel(
    tc, dy_words, dy_scales, a1, a3, w2_words, w2_scales, w1_words, w1_scales, w3_words, w3_scales,
    gate, offs, pos1, pos2, out,
):
    nc = tc.nc
    with ExitStack() as ctx:
        keep = ctx.enter_context(tc.tile_pool(name="keep", bufs=1))
        loads = ctx.enter_context(tc.tile_pool(name="loads", bufs=3))
        work = ctx.enter_context(tc.tile_pool(name="work", bufs=8))
        pairs = ctx.enter_context(tc.tile_pool(name="pairs", bufs=3))
        single = ctx.enter_context(tc.tile_pool(name="single", bufs=1))
        unit_pool = ctx.enter_context(tc.tile_pool(name="unit", bufs=2))
        psum_first = ctx.enter_context(tc.psum_pool(name="psum_first", bufs=3))
        psum_dh = ctx.enter_context(tc.psum_pool(name="psum_dh", bufs=4))
        psum_dx = ctx.enter_context(tc.psum_pool(name="psum_dx", bufs=1))

        offs_sb = keep.tile([P, SLOTS // LIST_ROWS], U16, name="offs_sb")
        pos1_sb = keep.tile([P, T // LIST_ROWS], U16, name="pos1_sb")
        pos2_sb = keep.tile([P, T // LIST_ROWS], U16, name="pos2_sb")
        dy_w = keep.tile([P, T], I32, name="dy_w", align_bytes=64)
        dy_s = keep.tile([P, T], U8, name="dy_s", align_bytes=64)
        w2_w = [keep.tile([P, 2 * H], U8, name="w2_w%d" % e, align_bytes=64) for e in range(E)]
        w2_s = keep.tile([P, E, H], U8, name="w2_s", align_bytes=64)
        w13_w = [keep.tile([P, UNITS, 2 * K], U8, name="w13_w%d" % m, align_bytes=64) for m in range(2)]
        w13_s = [keep.tile([P, UNITS, K], U8, name="w13_s%d" % m, align_bytes=64) for m in range(2)]
        g_w = keep.tile([P, SLOTS], U32, name="g_w", align_bytes=64)
        g_s = keep.tile([P, SLOTS], U8, name="g_s", align_bytes=64)
        ident = keep.tile([P, P], F32, name="ident")
        gate_rows = keep.tile([P, P], F32, name="gate_rows")
        gate_col = keep.tile([P, SLOTS // P], F32, name="gate_col")
        dx = keep.tile([P, SLOTS], F32, name="dx")

        nc.vector.memset(dy_s[:].bitcast(I32), 0)
        nc.vector.memset(w2_s[:].rearrange("p e i -> p (e i)").bitcast(I32), 0)
        nc.vector.memset(gate_rows[:], 0.0)
        for m in range(2):
            nc.vector.memset(w13_s[m][:].rearrange("p u k -> p (u k)").bitcast(I32), 0)
        make_identity(nc, ident[:])

        a_tiles = {}

        def load_saved(u, m):
            e, h = divmod(u, HALVES)
            a_tiles[u, m] = loads.tile([P, PACK, C], F32, name=("a1", "a3")[m])
            rows = (a1, a3)[m][h * PASS : (h + 1) * PASS, e * C : (e + 1) * C]
            nc.sync.dma_start(out=a_tiles[u, m][:], in_=rows.rearrange("(p t) n -> p t n", t=PACK))

        def load_w2(e):
            nc.sync.dma_start(out=w2_w[e][:].bitcast(I32), in_=w2_words[e, 0].bitcast(I32))

        def load_w2_scales(r):
            nc.sync.dma_start(
                out=w2_s[r:P:32, :, :].bitcast(I32),
                in_=w2_scales[:, 0, r:16:4, :].rearrange("e q i -> q e i").bitcast(I32),
            )

        nc.sync.dma_start(offs_sb[:], offs)
        nc.sync.dma_start(out=dy_w[:], in_=dy_words[0].rearrange("p n d -> p (n d)").bitcast(I32))
        load_saved(0, 0)
        for r in range(4):
            nc.sync.dma_start(out=dy_s[r:P:32, :].bitcast(I32), in_=dy_scales[0, r:16:4, :].bitcast(I32))
        nc.sync.dma_start(out=gate_rows[0 : SLOTS // P, :], in_=gate[0].rearrange("(c p) -> c p", p=P))
        for r in range(4):
            load_w2_scales(r)
        load_w2(0)
        load_saved(1, 0)
        load_saved(0, 1)
        load_w2(1)
        for m, (words, scales) in enumerate(((w1_words, w1_scales), (w3_words, w3_scales))):
            for r in range(4):
                nc.sync.dma_start(
                    out=w13_s[m][r:P:32, :, :].bitcast(I32),
                    in_=scales[:, :, r:16:4, :].rearrange("e s q k -> q (e s) k").bitcast(I32),
                )
        load_saved(1, 1)
        for m, (words, scales) in enumerate(((w1_words, w1_scales), (w3_words, w3_scales))):
            nc.sync.dma_start(out=w13_w[m][:].bitcast(I32), in_=words.rearrange("e s p b -> p (e s) b").bitcast(I32))
        load_saved(2, 0)
        for e in range(2, E):
            load_w2(e)
        nc.sync.dma_start(pos1_sb[:], pos1)
        nc.sync.dma_start(pos2_sb[:], pos2)

        def gather_words(lo, hi):
            cols = slice(lo // LIST_ROWS, hi // LIST_ROWS)
            nc.vector.tensor_copy(g_w[:, lo:hi], dy_w[:].bitcast(U32).indirect(offs_sb[:, cols]))

        def gather_scales(lo, hi):
            cols = slice(lo // LIST_ROWS, hi // LIST_ROWS)
            nc.vector.tensor_copy(g_s[:, lo:hi], dy_s[:].indirect(offs_sb[:, cols]))

        cuts = (0, C, C + 3 * T // 4, SLOTS)
        gather_words(cuts[0], cuts[1])
        gather_scales(cuts[0], cuts[1])

        half = C // 2
        turned = {}
        dh_banks = {}
        s_tiles = {}
        w_tiles = {}
        da3_tiles = {}
        code_tiles = {}
        da_tiles = {}
        dx_banks = {}

        def first_product(g):
            u, j = divmod(g, CHUNKS)
            e, h = divmod(u, HALVES)
            slots = slice(e * C + j * P, e * C + (j + 1) * P)
            bank = psum_first.tile([P, PASS], F32, name="first")
            nc.tensor.matmul_mx(
                out=bank[:],
                lhsT=g_w[:, slots].bitcast(E5M2),
                lhsT_scale=g_s[:, slots],
                rhs=w2_w[e][:, 2 * h * PASS : 2 * (h + 1) * PASS].bitcast(E2M1),
                rhs_scale=w2_s[:, e, h * PASS : (h + 1) * PASS],
                start=True,
                stop=True,
            )
            dh_t = work.tile([P, PACK, P], F32, name="dh_t")
            c = e * CHUNKS + j
            nc.scalar.activation(
                dh_t[:].rearrange("s t (r i) -> s r t i", i=2),
                bank[:].rearrange("s (r i t) -> s r t i", i=2, t=PACK),
                ACT.Copy,
                scale=gate_col[:, c : c + 1],
            )
            turned[g] = dh_t

        def turn(g):
            bank = psum_dh.tile([P, PACK, P], F32, name="dh")
            for t in range(PACK):
                nc.tensor.transpose(bank[:, t, :], turned[g][:, t, :], ident[:])
            dh_banks[g] = bank

        def sigmoid(u):
            s_tiles[u] = pairs.tile([P, PACK, C], F32, name="s")
            nc.scalar.activation(s_tiles[u][:], a_tiles[u, 0][:], ACT.Sigmoid, scale=-1.0)

        def times_a3(u, part):
            pool = (single, unit_pool)[part]
            engine = nc.gpsimd if part == 0 or u == 0 else nc.vector
            w_tiles[u, part] = pool.tile([P, PACK, half], F32, name="w")
            cols = slice(part * half, (part + 1) * half)
            engine.tensor_tensor(w_tiles[u, part][:], s_tiles[u][:, :, cols], a_tiles[u, 1][:, :, cols], ALU.mult)

        def make_da3(g):
            u, j = divmod(g, CHUNKS)
            if j == 0:
                da3_tiles[u] = unit_pool.tile([P, PACK, C], F32, name="da3")
                da_tiles[u] = unit_pool.tile([P, 2, C, PACK], BF16, name="da", align_bytes=64)
            cols = slice(j * P, (j + 1) * P)
            nc.vector.scalar_tensor_tensor(
                da3_tiles[u][:, :, cols], s_tiles[u][:, :, cols], 1.0, dh_banks[g][:], ALU.subtract, ALU.mult
            )

        def round_da3(u, lo, hi):
            nc.scalar.activation(
                da_tiles[u][:, 1, lo:hi, :].rearrange("p (c i) t -> p c t i", i=2),
                da3_tiles[u][:, :, lo:hi].rearrange("p t (c i) -> p c t i", i=2),
                ACT.Copy,
            )

        def make_da1(u, part):
            cols = slice(part * half, (part + 1) * half)
            nc.vector.tensor_tensor(
                da_tiles[u][:, 0, cols, :].rearrange("p (c i) t -> p c t i", i=2),
                da3_tiles[u][:, :, cols].rearrange("p t (c i) -> p c t i", i=2),
                w_tiles[u, part][:].rearrange("p t (c i) -> p c t i", i=2),
                ALU.mult,
            )

        def quantize(u, parts):
            if u not in code_tiles:
                codes = unit_pool.tile([P, 2 * C], U32, name="codes", align_bytes=64)
                scales = unit_pool.tile([P, 2 * C], U8, name="scales", align_bytes=64)
                code_tiles[u] = (codes, scales)
            codes, scales = code_tiles[u]
            values = da_tiles[u][:].rearrange("p m n t -> p (m n t)")
            for lo, hi in parts:
                nc.vector.quantize_mx(
                    out=codes[:, lo:hi].bitcast(E5M2), scales=scales[:, lo:hi], in_=values[:, PACK * lo : PACK * hi]
                )

        def second_product(u, m):
            e, h = divmod(u, HALVES)
            codes, scales = code_tiles[u]
            opens = h == 0 and m == 1
            closes = h == HALVES - 1 and m == 0
            if opens:
                dx_banks[e] = psum_dx.tile([K, C], F32, name="dx_bank")
            nc.tensor.matmul_mx(
                out=dx_banks[e][:],
                lhsT=w13_w[m][:, u, :].bitcast(E2M1),
                lhsT_scale=w13_s[m][:, u, :],
                rhs=codes[:, m * C : (m + 1) * C].bitcast(E5M2),
                rhs_scale=scales[:, m * C : (m + 1) * C],
                start=opens,
                stop=closes,
            )
            if closes:
                nc.scalar.activation(dx[:, e * C : (e + 1) * C], dx_banks[e][:], ACT.Copy)

        total = UNITS * CHUNKS
        last = UNITS - 1
        sigmoid(0)
        gate_bank = psum_dh.tile([P, PACK, P], F32, name="dh")
        nc.tensor.transpose(gate_bank[:, 0, :], gate_rows[:], ident[:])
        nc.scalar.activation(gate_col[:], gate_bank[:, 0, 0 : SLOTS // P], ACT.Copy, scale=-1.0)
        for lo, hi in zip(cuts[1:-1], cuts[2:]):
            gather_words(lo, hi)
            gather_scales(lo, hi)
        for g in range(CHUNKS):
            first_product(g)
            turn(g)
        sigmoid(1)
        for g in range(CHUNKS, 2 * CHUNKS):
            first_product(g)
        for u in range(UNITS):
            if u + 3 < UNITS:
                load_saved(u + 3, 0)
            if u + 2 < UNITS:
                load_saved(u + 2, 1)
            times_a3(u, 0)
            if u == 0:
                times_a3(u, 1)
            for g in range(u * CHUNKS, (u + 1) * CHUNKS):
                make_da3(g)
                if g + CHUNKS < total:
                    turn(g + CHUNKS)
                if u == last and g % 2 == 1:
                    round_da3(u, g % CHUNKS // 2 * half, (g % CHUNKS // 2 + 1) * half)
            if u + 2 < UNITS:
                sigmoid(u + 2)
            if u < last:
                round_da3(u, 0, C)
            for g in range((u + 2) * CHUNKS, min(total, (u + 3) * CHUNKS)):
                first_product(g)
            if u < last:
                times_a3(u + 1, 1)
            if u > 0:
                quantize(u - 1, [(0, 2 * C)])
                second_product(u - 1, 1)
                second_product(u - 1, 0)
            make_da1(u, 0)
            if u == last:
                quantize(u, [(C, 2 * C)])
                second_product(u, 1)
            make_da1(u, 1)
        quantize(last, [(0, half), (half, C)])
        second_product(last, 0)

        pieces = ((0, T // 2), (T // 2, T))
        fetched = {}

        def fetch(piece, m):
            lo, hi = pieces[piece]
            fetched[piece, m] = unit_pool.tile([P, hi - lo], F32, name=("first_slot", "second_slot")[m])
            offsets = (pos1_sb, pos2_sb)[m][:, lo // LIST_ROWS : hi // LIST_ROWS]
            nc.vector.tensor_copy(fetched[piece, m][:], dx[:].indirect(offsets))

        def add_and_store(piece):
            lo, hi = pieces[piece]
            both = fetched[piece, 0]
            nc.vector.tensor_tensor(both[:], both[:], fetched[piece, 1][:], ALU.add)
            nc.sync.dma_start(out=out[:, lo:hi], in_=both[:])

        fetch(0, 0)
        fetch(0, 1)
        fetch(1, 0)
        add_and_store(0)
        fetch(1, 1)
        add_and_store(1)
